import numpy as np
import ml_dtypes


def mxq(x, axis, fmt="e4m3"):
    dtype, down = {"e4m3": (ml_dtypes.float8_e4m3fn, 7), "e5m2": (ml_dtypes.float8_e5m2, 14)}[fmt]
    v = np.moveaxis(np.asarray(x, np.float32).astype(ml_dtypes.bfloat16).astype(np.float64), axis, -1)
    blocks = v.reshape(v.shape[:-1] + (-1, 32))
    amax = np.abs(blocks).max(-1, keepdims=True)
    byte = np.maximum(np.where(amax > 0, np.frexp(amax)[1] - 1 + 127, 0) - down, 1)
    scale = np.exp2(byte - 127.0)
    codes = (blocks / scale).astype(np.float32).astype(dtype).astype(np.float64)
    return np.moveaxis((codes * scale).reshape(v.shape), -1, axis)


WIDE = False


def mx_kscale(k):
    if not WIDE:
        return np.ones(k)
    levels = np.array([10, -10, 5, -5, 0])
    if k % 512:
        return np.exp2(np.random.permutation(np.resize(levels, k // 32))).repeat(32)
    a = np.empty((k // 512, 16))
    for p in range(k // 512):
        a[p, :8] = np.random.permutation(np.resize(levels, 8))
        for g in range(8):
            far = levels[np.abs(levels - a[p, g]) >= 10]
            a[p, g + 8] = far[np.random.randint(len(far))]
    return np.exp2(a.ravel()).repeat(32)


def f64(x):
    return np.asarray(x).astype(np.float64)


def striped(idx):
    return np.tile(np.asarray(idx).reshape(-1, 16).T, (8, 1)).astype(np.uint16)


def unstriped(offs):
    return offs[:16].T.reshape(-1).astype(np.int64)


D, T, I, Q, U, G, M = 512, 2048, 512, 128, 1024, 64, 512


def setup_inputs():
    n = np.random.standard_normal
    idx = np.random.permutation(T)[:I]
    idx2 = np.random.permutation(U)[:I]
    idx3 = np.random.permutation(M)[:G]
    fd = mx_kscale(D)
    return {
        "query": (n((D, Q)) * 0.9 / np.sqrt(D) * fd[:, None]).astype(np.float32),
        "keys": (n((D, T)) / fd[:, None]).astype(np.float32),
        "notes": (n((D, U)) / fd[:, None]).astype(np.float32),
        "worth": np.tile(np.random.uniform(0.2, 2.0, T), (128, 1)).astype(np.float32),
        "old": (1.0 * n((Q, M))).astype(np.float32),
        "offs": striped(idx),
        "offs2": striped(idx2),
        "offs3": striped(idx3),
    }


def reference(query, keys, notes, worth, old, offs, offs2, offs3):
    idx = unstriped(offs)
    idx2 = unstriped(offs2)
    idx3 = unstriped(offs3)
    zk = np.abs(f64(keys)[:, idx] - f64(notes)[:, idx2])
    queryq = mxq(f64(query), 0, "e4m3")
    zkq = mxq(zk, 0, "e4m3")
    s = queryq.T @ zkq
    w = np.maximum(s, 0.0)
    ws = w * f64(worth)[:1][:, idx] * 2.0
    wp = ws.reshape(Q, G, I // G).sum(axis=2)
    wf = np.zeros((Q, M))
    wf[:, idx3] = wp
    y = f64(old) + wf
    return y

@@ -1,0 +1,141 @@
+from contextlib import ExitStack
+
+import concourse.mybir as mybir
+from concourse.masks import make_identity
+
+D, T, I, Q, U, G, M = 512, 2048, 512, 128, 1024, 64, 512
+FLOPS = 2 * D * Q * I
+
+F32 = mybir.dt.float32
+BF16 = mybir.dt.bfloat16
+U32 = mybir.dt.uint32
+U16 = mybir.dt.uint16
+U8 = mybir.dt.uint8
+FP8X4 = mybir.dt.float8_e4m3fn_x4
+ALU = mybir.AluOpType
+ACT = mybir.ActivationFunctionType
+
+P = 128
+PACK = 4
+RUN = I // G
+PER_COL = 16
+CHUNKS = ((0, 256), (256, 512))
+
+
+def tile_attend_keyapart_pagesums_lean_kernel(tc, query, keys, notes, worth, old, offs, offs2, offs3, out):
+    nc = tc.nc
+    with ExitStack() as ctx:
+        sb = ctx.enter_context(tc.tile_pool(name="sb", bufs=1))
+        ps = ctx.enter_context(tc.psum_pool(name="ps", bufs=1))
+
+        key_rows = keys.rearrange("(p j) t -> p j t", j=PACK)
+        note_rows = notes.rearrange("(p j) u -> p j u", j=PACK)
+
+        idx = sb.tile([P, I // PER_COL], U16, name="idx")
+        idx2 = sb.tile([P, I // PER_COL], U16, name="idx2")
+        idx3 = sb.tile([P, G // PER_COL], U16, name="idx3")
+        key_sb = [sb.tile([P, T], F32, name=f"key{j}") for j in range(PACK)]
+        note_sb = [sb.tile([P, 2, U], F32, name=f"note{h}") for h in range(2)]
+        worth_col = sb.tile([P, T // P], F32, name="worth_col")
+        q_raw = sb.tile([P, PACK, Q], F32, name="q_raw")
+        old_sb = sb.tile([P, M], F32, name="old_sb")
+
+        nc.sync.dma_start(out=worth_col[:], in_=worth[0, :].rearrange("(p j) -> p j", p=P))
+        nc.sync.dma_start(out=note_sb[0][:], in_=note_rows[:, 0:2, :])
+        nc.sync.dma_start(idx2[:], offs2)
+        nc.sync.dma_start(idx[:], offs)
+        nc.sync.dma_start(out=key_sb[0][:], in_=key_rows[:, 0, :])
+        nc.sync.dma_start(out=key_sb[1][:], in_=key_rows[:, 1, :])
+        nc.sync.dma_start(out=note_sb[1][:], in_=note_rows[:, 2:4, :])
+        nc.sync.dma_start(out=q_raw[:], in_=query.rearrange("(p j) q -> p j q", j=PACK))
+        nc.sync.dma_start(out=key_sb[2][:], in_=key_rows[:, 2, :])
+        nc.sync.dma_start(out=key_sb[3][:], in_=key_rows[:, 3, :])
+        nc.sync.dma_start(idx3[:], offs3)
+        nc.sync.dma_start(out=old_sb[:], in_=old)
+
+        ident = sb.tile([P, P], F32, name="ident")
+        make_identity(nc, ident[:])
+        placed = sb.tile([P, M], F32, name="placed")
+        nc.gpsimd.memset(placed[:], 0.0)
+
+        worth_sb = sb.tile([P, T], F32, name="worth_sb")
+        worth_view = worth_sb[:].rearrange("m (p j) -> m p j", p=P)
+        for b in range(T // P // 4):
+            bank = ps.tile([P, 4, P], F32, name=f"wbank{b}")
+            for j in range(4):
+                col = 4 * b + j
+                nc.tensor.transpose(bank[:, j, :], worth_col[:, col : col + 1].to_broadcast([P, P]), ident[:])
+            nc.vector.tensor_copy(out=worth_view[:, :, 4 * b : 4 * b + 4], in_=bank[:].rearrange("m j p -> m p j"))
+        worth2 = sb.tile([P, I], F32, name="worth2")
+        nc.vector.tensor_scalar(worth2[:], worth_sb[:].indirect(idx[:]), 2.0, 0.0, ALU.mult, ALU.add)
+
+        picked = [sb.tile([P, I], F32, name=f"picked{j}") for j in range(PACK)]
+        diff = [sb.tile([P, 2, I], F32, name=f"diff{h}") for h in range(2)]
+        zk = [sb.tile([P, b - a, PACK], BF16, name=f"zk{a}", align_bytes=64) for a, b in CHUNKS]
+
+        def gather_notes(j):
+            nc.scalar.activation(picked[j][:], note_sb[j // 2][:, j % 2, :].indirect(idx2[:]), ACT.Copy)
+
+        def subtract(j, a, b):
+            nc.vector.tensor_tensor(
+                diff[j // 2][:, j % 2, a:b],
+                key_sb[j][:].indirect(idx[:, a // PER_COL : b // PER_COL]),
+                picked[j][:, a:b],
+                ALU.subtract,
+            )
+
+        def absolute(h, c):
+            a, b = CHUNKS[c]
+            nc.scalar.activation(
+                zk[c][:, :, 2 * h : 2 * h + 2], diff[h][:, :, a:b].rearrange("p j s -> p s j"), ACT.Abs
+            )
+
+        gather_notes(0)
+        gather_notes(1)
+        subtract(0, 0, I)
+        subtract(1, 0, I)
+        gather_notes(2)
+        gather_notes(3)
+        for c in range(len(CHUNKS)):
+            absolute(0, c)
+
+        q_bf = sb.tile([P, Q, PACK], BF16, name="q_bf", align_bytes=64)
+        q_codes = sb.tile([P, Q], U32, name="q_codes", align_bytes=64)
+        q_scales = sb.tile([P, Q], U8, name="q_scales", align_bytes=64)
+        nc.vector.tensor_copy(out=q_bf[:], in_=q_raw[:].rearrange("p j q -> p q j"))
+        subtract(2, 0, I)
+        nc.vector.quantize_mx(out=q_codes[:].bitcast(FP8X4), scales=q_scales[:], in_=q_bf[:].rearrange("p q j -> p (q j)"))
+
+        for a, b in CHUNKS:
+            subtract(3, a, b)
+        for c in range(len(CHUNKS)):
+            absolute(1, c)
+
+        sums = sb.tile([P, G], F32, name="sums")
+        scores = []
+        for c, (a, b) in enumerate(CHUNKS):
+            codes = sb.tile([P, b - a], U32, name=f"codes{c}", align_bytes=64)
+            scales = sb.tile([P, b - a], U8, name=f"scales{c}", align_bytes=64)
+            nc.vector.quantize_mx(out=codes[:].bitcast(FP8X4), scales=scales[:], in_=zk[c][:].rearrange("p s j -> p (s j)"))
+            s = ps.tile([P, b - a], F32, name=f"s{c}")
+            nc.tensor.matmul_mx(
+                out=s[:],
+                lhsT=q_codes[:].bitcast(FP8X4),
+                lhsT_scale=q_scales[:],
+                rhs=codes[:].bitcast(FP8X4),
+                rhs_scale=scales[:],
+                start=True,
+                stop=True,
+            )
+            scores.append(s)
+        for c, (a, b) in enumerate(CHUNKS):
+            ws = sb.tile([P, b - a], F32, name=f"ws{c}")
+            nc.vector.scalar_tensor_tensor(ws[:], scores[c][:], 0.0, worth2[:, a:b], ALU.max, ALU.mult)
+            nc.vector.tensor_reduce(
+                sums[:, a // RUN : b // RUN], ws[:].rearrange("p (g r) -> p g r", r=RUN), mybir.AxisListType.X, ALU.add
+            )
+
+        nc.vector.tensor_copy(placed[:].indirect(idx3[:]), sums[:])
+        result = sb.tile([P, M], F32, name="result")
+        nc.vector.tensor_tensor(result[:], old_sb[:], placed[:], ALU.add)
+        nc.sync.dma_start(out=out, in_=result[:])

@@ -19,7 +19,7 @@ P = 128
 PACK = 4
 RUN = I // G
 PER_COL = 16
-CHUNKS = ((0, 256), (256, 512))
+CHUNKS = ((0, 128), (128, 256), (256, 384), (384, 512))
 
 
 def tile_attend_keyapart_pagesums_lean_kernel(tc, query, keys, notes, worth, old, offs, offs2, offs3, out):
@@ -40,14 +40,14 @@ def tile_attend_keyapart_pagesums_lean_kernel(tc, query, keys, notes, worth, old
         q_raw = sb.tile([P, PACK, Q], F32, name="q_raw")
         old_sb = sb.tile([P, M], F32, name="old_sb")
 
-        nc.sync.dma_start(out=worth_col[:], in_=worth[0, :].rearrange("(p j) -> p j", p=P))
+        nc.scalar.dma_start(out=worth_col[:], in_=worth[0, :].rearrange("(p j) -> p j", p=P))
         nc.sync.dma_start(out=note_sb[0][:], in_=note_rows[:, 0:2, :])
         nc.sync.dma_start(idx2[:], offs2)
         nc.sync.dma_start(idx[:], offs)
-        nc.sync.dma_start(out=key_sb[0][:], in_=key_rows[:, 0, :])
-        nc.sync.dma_start(out=key_sb[1][:], in_=key_rows[:, 1, :])
         nc.sync.dma_start(out=note_sb[1][:], in_=note_rows[:, 2:4, :])
+        nc.sync.dma_start(out=key_sb[0][:], in_=key_rows[:, 0, :])
         nc.sync.dma_start(out=q_raw[:], in_=query.rearrange("(p j) q -> p j q", j=PACK))
+        nc.sync.dma_start(out=key_sb[1][:], in_=key_rows[:, 1, :])
         nc.sync.dma_start(out=key_sb[2][:], in_=key_rows[:, 2, :])
         nc.sync.dma_start(out=key_sb[3][:], in_=key_rows[:, 3, :])
         nc.sync.dma_start(idx3[:], offs3)
@@ -58,7 +58,7 @@ def tile_attend_keyapart_pagesums_lean_kernel(tc, query, keys, notes, worth, old
         placed = sb.tile([P, M], F32, name="placed")
         nc.gpsimd.memset(placed[:], 0.0)
 
-        worth_sb = sb.tile([P, T], F32, name="worth_sb")
+        worth_sb = sb.tile([P, T], F32, name="worth_sb", tag="first", align_bytes=64)
         worth_view = worth_sb[:].rearrange("m (p j) -> m p j", p=P)
         for b in range(T // P // 4):
             bank = ps.tile([P, 4, P], F32, name=f"wbank{b}")
@@ -70,7 +70,13 @@ def tile_attend_keyapart_pagesums_lean_kernel(tc, query, keys, notes, worth, old
         nc.vector.tensor_scalar(worth2[:], worth_sb[:].indirect(idx[:]), 2.0, 0.0, ALU.mult, ALU.add)
 
         picked = [sb.tile([P, I], F32, name=f"picked{j}") for j in range(PACK)]
-        diff = [sb.tile([P, 2, I], F32, name=f"diff{h}") for h in range(2)]
+        q_bf = sb.tile([P, Q, PACK], BF16, name="q_bf", tag="second", align_bytes=64)
+        q_codes = sb.tile([P, Q], U32, name="q_codes", align_bytes=64)
+        q_scales = sb.tile([P, Q], U8, name="q_scales", align_bytes=64)
+        nc.vector.tensor_copy(out=q_bf[:], in_=q_raw[:].rearrange("p j q -> p q j"))
+        nc.vector.quantize_mx(out=q_codes[:].bitcast(FP8X4), scales=q_scales[:], in_=q_bf[:].rearrange("p q j -> p (q j)"))
+
+        diff = [sb.tile([P, 2, I], F32, name=f"diff{h}", tag=("first", "second")[h], align_bytes=64) for h in range(2)]
         zk = [sb.tile([P, b - a, PACK], BF16, name=f"zk{a}", align_bytes=64) for a, b in CHUNKS]
 
         def gather_notes(j):
@@ -90,22 +96,13 @@ def tile_attend_keyapart_pagesums_lean_kernel(tc, query, keys, notes, worth, old
                 zk[c][:, :, 2 * h : 2 * h + 2], diff[h][:, :, a:b].rearrange("p j s -> p s j"), ACT.Abs
             )
 
-        gather_notes(0)
-        gather_notes(1)
+        for j in range(PACK):
+            gather_notes(j)
         subtract(0, 0, I)
         subtract(1, 0, I)
-        gather_notes(2)
-        gather_notes(3)
         for c in range(len(CHUNKS)):
             absolute(0, c)
-
-        q_bf = sb.tile([P, Q, PACK], BF16, name="q_bf", align_bytes=64)
-        q_codes = sb.tile([P, Q], U32, name="q_codes", align_bytes=64)
-        q_scales = sb.tile([P, Q], U8, name="q_scales", align_bytes=64)
-        nc.vector.tensor_copy(out=q_bf[:], in_=q_raw[:].rearrange("p j q -> p q j"))
         subtract(2, 0, I)
-        nc.vector.quantize_mx(out=q_codes[:].bitcast(FP8X4), scales=q_scales[:], in_=q_bf[:].rearrange("p q j -> p (q j)"))
-
         for a, b in CHUNKS:
             subtract(3, a, b)
         for c in range(len(CHUNKS)):
@@ -136,6 +133,8 @@ def tile_attend_keyapart_pagesums_lean_kernel(tc, query, keys, notes, worth, old
             )
 
         nc.vector.tensor_copy(placed[:].indirect(idx3[:]), sums[:])
-        result = sb.tile([P, M], F32, name="result")
-        nc.vector.tensor_tensor(result[:], old_sb[:], placed[:], ALU.add)
-        nc.sync.dma_start(out=out, in_=result[:])
+        for h, queue in enumerate((nc.scalar, nc.sync)):
+            cols = slice(h * M // 2, (h + 1) * M // 2)
+            result = sb.tile([P, M // 2], F32, name=f"result{h}")
+            nc.vector.tensor_tensor(result[:], old_sb[:, cols], placed[:, cols], ALU.add)
+            queue.dma_start(out=out[:, cols], in_=result[:])

@@ -17,9 +17,19 @@ ACT = mybir.ActivationFunctionType
 
 P = 128
 PACK = 4
+PAIR = 2
 RUN = I // G
-PER_COL = 16
-CHUNKS = ((0, 128), (128, 256), (256, 384), (384, 512))
+LIST_ROWS = 16
+BANK_COLS = 512
+LINE = 4
+HALF = I // 2
+
+CHUNKS = ((0, 128), (128, 256), (256, 384), (384, 448), (448, 512))
+SCALAR_FROM = 384
+
+
+def list_slice(tile, a, b):
+    return tile[:, a // LIST_ROWS : b // LIST_ROWS]
 
 
 def tile_attend_keyapart_pagesums_lean_kernel(tc, query, keys, notes, worth, old, offs, offs2, offs3, out):
@@ -28,28 +38,26 @@ def tile_attend_keyapart_pagesums_lean_kernel(tc, query, keys, notes, worth, old
         sb = ctx.enter_context(tc.tile_pool(name="sb", bufs=1))
         ps = ctx.enter_context(tc.psum_pool(name="ps", bufs=1))
 
-        key_rows = keys.rearrange("(p j) t -> p j t", j=PACK)
-        note_rows = notes.rearrange("(p j) u -> p j u", j=PACK)
+        key_rows = keys.rearrange("(p t) c -> p t c", t=PACK)
+        note_rows = notes.rearrange("(p t) c -> p t c", t=PACK)
 
-        idx = sb.tile([P, I // PER_COL], U16, name="idx")
-        idx2 = sb.tile([P, I // PER_COL], U16, name="idx2")
-        idx3 = sb.tile([P, G // PER_COL], U16, name="idx3")
-        key_sb = [sb.tile([P, T], F32, name=f"key{j}") for j in range(PACK)]
-        note_sb = [sb.tile([P, 2, U], F32, name=f"note{h}") for h in range(2)]
-        worth_col = sb.tile([P, T // P], F32, name="worth_col")
+        idx = sb.tile([P, I // LIST_ROWS], U16, name="idx")
+        idx2 = sb.tile([P, I // LIST_ROWS], U16, name="idx2")
+        idx3 = sb.tile([P, G // LIST_ROWS], U16, name="idx3")
+        key_plane = [sb.tile([P, T], F32, name=f"key_plane{t}") for t in range(PACK)]
+        note_pair = [sb.tile([P, PAIR, U], F32, name=f"note_pair{h}") for h in range(PACK // PAIR)]
+        worth_cols = sb.tile([P, T // P], F32, name="worth_cols")
         q_raw = sb.tile([P, PACK, Q], F32, name="q_raw")
         old_sb = sb.tile([P, M], F32, name="old_sb")
 
-        nc.scalar.dma_start(out=worth_col[:], in_=worth[0, :].rearrange("(p j) -> p j", p=P))
-        nc.sync.dma_start(out=note_sb[0][:], in_=note_rows[:, 0:2, :])
+        nc.scalar.dma_start(out=worth_cols[:], in_=worth[0, :].rearrange("(p j) -> p j", p=P))
+        nc.sync.dma_start(out=note_pair[0][:], in_=note_rows[:, 0:PAIR, :])
         nc.sync.dma_start(idx2[:], offs2)
         nc.sync.dma_start(idx[:], offs)
-        nc.sync.dma_start(out=note_sb[1][:], in_=note_rows[:, 2:4, :])
-        nc.sync.dma_start(out=key_sb[0][:], in_=key_rows[:, 0, :])
-        nc.sync.dma_start(out=q_raw[:], in_=query.rearrange("(p j) q -> p j q", j=PACK))
-        nc.sync.dma_start(out=key_sb[1][:], in_=key_rows[:, 1, :])
-        nc.sync.dma_start(out=key_sb[2][:], in_=key_rows[:, 2, :])
-        nc.sync.dma_start(out=key_sb[3][:], in_=key_rows[:, 3, :])
+        nc.sync.dma_start(out=note_pair[1][:], in_=note_rows[:, PAIR:PACK, :])
+        for t in range(PACK):
+            nc.sync.dma_start(out=key_plane[t][:], in_=key_rows[:, t, :])
+        nc.sync.dma_start(out=q_raw[:], in_=query.rearrange("(p t) q -> p t q", t=PACK))
         nc.sync.dma_start(idx3[:], offs3)
         nc.sync.dma_start(out=old_sb[:], in_=old)
 
@@ -58,65 +66,88 @@ def tile_attend_keyapart_pagesums_lean_kernel(tc, query, keys, notes, worth, old
         placed = sb.tile([P, M], F32, name="placed")
         nc.gpsimd.memset(placed[:], 0.0)
 
-        worth_sb = sb.tile([P, T], F32, name="worth_sb", tag="first", align_bytes=64)
-        worth_view = worth_sb[:].rearrange("m (p j) -> m p j", p=P)
-        for b in range(T // P // 4):
-            bank = ps.tile([P, 4, P], F32, name=f"wbank{b}")
-            for j in range(4):
-                col = 4 * b + j
-                nc.tensor.transpose(bank[:, j, :], worth_col[:, col : col + 1].to_broadcast([P, P]), ident[:])
-            nc.vector.tensor_copy(out=worth_view[:, :, 4 * b : 4 * b + 4], in_=bank[:].rearrange("m j p -> m p j"))
+        worth_all = sb.tile([P, T], F32, name="worth_all", tag="early", align_bytes=64)
+        worth_view = worth_all[:].rearrange("m (p j) -> m p j", p=P)
+        per_bank = BANK_COLS // P
+        for b in range(T // BANK_COLS):
+            spread = ps.tile([P, per_bank, P], F32, name=f"spread{b}", tag=f"bank{b}")
+            for j in range(per_bank):
+                col = per_bank * b + j
+                nc.tensor.transpose(spread[:, j, :], worth_cols[:, col : col + 1].to_broadcast([P, P]), ident[:])
+            nc.vector.tensor_copy(
+                out=worth_view[:, :, per_bank * b : per_bank * (b + 1)], in_=spread[:].rearrange("m j p -> m p j")
+            )
         worth2 = sb.tile([P, I], F32, name="worth2")
-        nc.vector.tensor_scalar(worth2[:], worth_sb[:].indirect(idx[:]), 2.0, 0.0, ALU.mult, ALU.add)
+        nc.vector.tensor_scalar(worth2[:], worth_all[:].indirect(idx[:]), 2.0, 0.0, ALU.mult, ALU.add)
 
-        picked = [sb.tile([P, I], F32, name=f"picked{j}") for j in range(PACK)]
-        q_bf = sb.tile([P, Q, PACK], BF16, name="q_bf", tag="second", align_bytes=64)
-        q_codes = sb.tile([P, Q], U32, name="q_codes", align_bytes=64)
-        q_scales = sb.tile([P, Q], U8, name="q_scales", align_bytes=64)
-        nc.vector.tensor_copy(out=q_bf[:], in_=q_raw[:].rearrange("p j q -> p q j"))
-        nc.vector.quantize_mx(out=q_codes[:].bitcast(FP8X4), scales=q_scales[:], in_=q_bf[:].rearrange("p q j -> p (q j)"))
-
-        diff = [sb.tile([P, 2, I], F32, name=f"diff{h}", tag=("first", "second")[h], align_bytes=64) for h in range(2)]
+        picked = [sb.tile([P, I], F32, name=f"picked{t}") for t in range(PACK - 1)]
+        picked_last = [
+            sb.tile([P, HALF], F32, name=f"picked_last{h}", tag=f"picked_last{h}", align_bytes=64) for h in range(2)
+        ]
+        diff = [
+            sb.tile([P, PAIR, I], F32, name=f"diff{h}", tag=("early", "late")[h], align_bytes=64)
+            for h in range(PACK // PAIR)
+        ]
         zk = [sb.tile([P, b - a, PACK], BF16, name=f"zk{a}", align_bytes=64) for a, b in CHUNKS]
 
-        def gather_notes(j):
-            nc.scalar.activation(picked[j][:], note_sb[j // 2][:, j % 2, :].indirect(idx2[:]), ACT.Copy)
+        def absolute(h):
+            for c, (a, b) in enumerate(CHUNKS):
+                nc.scalar.activation(
+                    zk[c][:, :, PAIR * h : PAIR * (h + 1)], diff[h][:, :, a:b].rearrange("p t s -> p s t"), ACT.Abs
+                )
 
-        def subtract(j, a, b):
+        def last_notes(a, b):
+            return picked_last[a // HALF][:, a % HALF : a % HALF + b - a]
+
+        for t in range(PACK - 1):
+            nc.scalar.activation(picked[t][:], note_pair[t // PAIR][:, t % PAIR, :].indirect(idx2[:]), ACT.Copy)
+        for h in range(2):
+            listed = list_slice(idx2, h * HALF, (h + 1) * HALF)
+            nc.scalar.activation(picked_last[h][:], note_pair[-1][:, PAIR - 1, :].indirect(listed), ACT.Copy)
+        for t in range(PACK - 1):
             nc.vector.tensor_tensor(
-                diff[j // 2][:, j % 2, a:b],
-                key_sb[j][:].indirect(idx[:, a // PER_COL : b // PER_COL]),
-                picked[j][:, a:b],
-                ALU.subtract,
+                diff[t // PAIR][:, t % PAIR, :], key_plane[t][:].indirect(idx[:]), picked[t][:], ALU.subtract
             )
+            if t == PAIR - 1:
+                absolute(0)
 
-        def absolute(h, c):
-            a, b = CHUNKS[c]
-            nc.scalar.activation(
-                zk[c][:, :, 2 * h : 2 * h + 2], diff[h][:, :, a:b].rearrange("p j s -> p s j"), ACT.Abs
-            )
-
-        for j in range(PACK):
-            gather_notes(j)
-        subtract(0, 0, I)
-        subtract(1, 0, I)
-        for c in range(len(CHUNKS)):
-            absolute(0, c)
-        subtract(2, 0, I)
+        last_keys = sb.tile([P, I - SCALAR_FROM], F32, name="last_keys")
+        nc.scalar.activation(last_keys[:], key_plane[-1][:].indirect(list_slice(idx, SCALAR_FROM, I)), ACT.Copy)
         for a, b in CHUNKS:
-            subtract(3, a, b)
-        for c in range(len(CHUNKS)):
-            absolute(1, c)
+            if b <= SCALAR_FROM:
+                nc.vector.tensor_tensor(
+                    diff[-1][:, PAIR - 1, a:b],
+                    key_plane[-1][:].indirect(list_slice(idx, a, b)),
+                    last_notes(a, b),
+                    ALU.subtract,
+                )
+        nc.vector.tensor_tensor(
+            diff[-1][:, PAIR - 1, SCALAR_FROM:I], last_keys[:], last_notes(SCALAR_FROM, I), ALU.subtract
+        )
 
-        sums = sb.tile([P, G], F32, name="sums")
+        q_bf = sb.tile([P, Q, PACK], BF16, name="q_bf", tag="picked_last0", align_bytes=64)
+        q_codes = sb.tile([P, Q], U32, name="q_codes", align_bytes=64)
+        q_scales = sb.tile([P, Q], U8, name="q_scales", align_bytes=64)
+        nc.vector.tensor_copy(
+            out=q_bf[:].rearrange("p (c i) t -> p c t i", i=LINE),
+            in_=q_raw[:].rearrange("p t (c i) -> p c t i", i=LINE),
+        )
+        nc.vector.quantize_mx(
+            out=q_codes[:].bitcast(FP8X4), scales=q_scales[:], in_=q_bf[:].rearrange("p q t -> p (q t)")
+        )
+
+        absolute(1)
+
         scores = []
         for c, (a, b) in enumerate(CHUNKS):
             codes = sb.tile([P, b - a], U32, name=f"codes{c}", align_bytes=64)
             scales = sb.tile([P, b - a], U8, name=f"scales{c}", align_bytes=64)
-            nc.vector.quantize_mx(out=codes[:].bitcast(FP8X4), scales=scales[:], in_=zk[c][:].rearrange("p s j -> p (s j)"))
-            s = ps.tile([P, b - a], F32, name=f"s{c}")
+            nc.vector.quantize_mx(
+                out=codes[:].bitcast(FP8X4), scales=scales[:], in_=zk[c][:].rearrange("p s t -> p (s t)")
+            )
+            score = ps.tile([P, b - a], F32, name=f"score{c}", tag=f"bank{c}")
             nc.tensor.matmul_mx(
-                out=s[:],
+                out=score[:],
                 lhsT=q_codes[:].bitcast(FP8X4),
                 lhsT_scale=q_scales[:],
                 rhs=codes[:].bitcast(FP8X4),
@@ -124,12 +155,17 @@ def tile_attend_keyapart_pagesums_lean_kernel(tc, query, keys, notes, worth, old
                 start=True,
                 stop=True,
             )
-            scores.append(s)
+            scores.append(score)
+
+        sums = sb.tile([P, G], F32, name="sums")
         for c, (a, b) in enumerate(CHUNKS):
-            ws = sb.tile([P, b - a], F32, name=f"ws{c}")
-            nc.vector.scalar_tensor_tensor(ws[:], scores[c][:], 0.0, worth2[:, a:b], ALU.max, ALU.mult)
+            weighted = sb.tile([P, b - a], F32, name=f"weighted{c}")
+            nc.vector.scalar_tensor_tensor(weighted[:], scores[c][:], 0.0, worth2[:, a:b], ALU.max, ALU.mult)
             nc.vector.tensor_reduce(
-                sums[:, a // RUN : b // RUN], ws[:].rearrange("p (g r) -> p g r", r=RUN), mybir.AxisListType.X, ALU.add
+                sums[:, a // RUN : b // RUN],
+                weighted[:].rearrange("p (g r) -> p g r", r=RUN),
+                mybir.AxisListType.X,
+                ALU.add,
             )
 
         nc.vector.tensor_copy(placed[:].indirect(idx3[:]), sums[:])

from contextlib import ExitStack

import concourse.mybir as mybir
from concourse.masks import make_identity

D, T, I, Q, U, G, M = 512, 2048, 512, 128, 1024, 64, 512
FLOPS = 2 * D * Q * I

F32 = mybir.dt.float32
BF16 = mybir.dt.bfloat16
U32 = mybir.dt.uint32
U16 = mybir.dt.uint16
U8 = mybir.dt.uint8
FP8X4 = mybir.dt.float8_e4m3fn_x4
ALU = mybir.AluOpType
ACT = mybir.ActivationFunctionType

P = 128
PACK = 4
PAIR = 2
RUN = I // G
LIST_ROWS = 16
BANK_COLS = 512
LINE = 4
HALF = I // 2

CHUNKS = ((0, 128), (128, 256), (256, 384), (384, 448), (448, 512))
SCALAR_FROM = 384


def list_slice(tile, a, b):
    return tile[:, a // LIST_ROWS : b // LIST_ROWS]


def tile_attend_keyapart_pagesums_lean_kernel(tc, query, keys, notes, worth, old, offs, offs2, offs3, out):
    nc = tc.nc
    with ExitStack() as ctx:
        sb = ctx.enter_context(tc.tile_pool(name="sb", bufs=1))
        ps = ctx.enter_context(tc.psum_pool(name="ps", bufs=1))

        key_rows = keys.rearrange("(p t) c -> p t c", t=PACK)
        note_rows = notes.rearrange("(p t) c -> p t c", t=PACK)

        idx = sb.tile([P, I // LIST_ROWS], U16, name="idx")
        idx2 = sb.tile([P, I // LIST_ROWS], U16, name="idx2")
        idx3 = sb.tile([P, G // LIST_ROWS], U16, name="idx3")
        key_plane = [sb.tile([P, T], F32, name=f"key_plane{t}") for t in range(PACK)]
        note_pair = [sb.tile([P, PAIR, U], F32, name=f"note_pair{h}") for h in range(PACK // PAIR)]
        worth_cols = sb.tile([P, T // P], F32, name="worth_cols")
        q_raw = sb.tile([P, PACK, Q], F32, name="q_raw")
        old_sb = sb.tile([P, M], F32, name="old_sb")

        nc.scalar.dma_start(out=worth_cols[:], in_=worth[0, :].rearrange("(p j) -> p j", p=P))
        nc.sync.dma_start(out=note_pair[0][:], in_=note_rows[:, 0:PAIR, :])
        nc.sync.dma_start(idx2[:], offs2)
        nc.sync.dma_start(idx[:], offs)
        nc.sync.dma_start(out=note_pair[1][:], in_=note_rows[:, PAIR:PACK, :])
        for t in range(PACK):
            nc.sync.dma_start(out=key_plane[t][:], in_=key_rows[:, t, :])
        nc.sync.dma_start(out=q_raw[:], in_=query.rearrange("(p t) q -> p t q", t=PACK))
        nc.sync.dma_start(idx3[:], offs3)
        nc.sync.dma_start(out=old_sb[:], in_=old)

        ident = sb.tile([P, P], F32, name="ident")
        make_identity(nc, ident[:])
        placed = sb.tile([P, M], F32, name="placed")
        nc.gpsimd.memset(placed[:], 0.0)

        worth_all = sb.tile([P, T], F32, name="worth_all", tag="early", align_bytes=64)
        worth_view = worth_all[:].rearrange("m (p j) -> m p j", p=P)
        per_bank = BANK_COLS // P
        for b in range(T // BANK_COLS):
            spread = ps.tile([P, per_bank, P], F32, name=f"spread{b}", tag=f"bank{b}")
            for j in range(per_bank):
                col = per_bank * b + j
                nc.tensor.transpose(spread[:, j, :], worth_cols[:, col : col + 1].to_broadcast([P, P]), ident[:])
            nc.vector.tensor_copy(
                out=worth_view[:, :, per_bank * b : per_bank * (b + 1)], in_=spread[:].rearrange("m j p -> m p j")
            )
        worth2 = sb.tile([P, I], F32, name="worth2")
        nc.vector.tensor_scalar(worth2[:], worth_all[:].indirect(idx[:]), 2.0, 0.0, ALU.mult, ALU.add)

        picked = [sb.tile([P, I], F32, name=f"picked{t}") for t in range(PACK - 1)]
        picked_last = [
            sb.tile([P, HALF], F32, name=f"picked_last{h}", tag=f"picked_last{h}", align_bytes=64) for h in range(2)
        ]
        diff = [
            sb.tile([P, PAIR, I], F32, name=f"diff{h}", tag=("early", "late")[h], align_bytes=64)
            for h in range(PACK // PAIR)
        ]
        zk = [sb.tile([P, b - a, PACK], BF16, name=f"zk{a}", align_bytes=64) for a, b in CHUNKS]

        def absolute(h):
            for c, (a, b) in enumerate(CHUNKS):
                nc.scalar.activation(
                    zk[c][:, :, PAIR * h : PAIR * (h + 1)], diff[h][:, :, a:b].rearrange("p t s -> p s t"), ACT.Abs
                )

        def last_notes(a, b):
            return picked_last[a // HALF][:, a % HALF : a % HALF + b - a]

        for t in range(PACK - 1):
            nc.scalar.activation(picked[t][:], note_pair[t // PAIR][:, t % PAIR, :].indirect(idx2[:]), ACT.Copy)
        for h in range(2):
            listed = list_slice(idx2, h * HALF, (h + 1) * HALF)
            nc.scalar.activation(picked_last[h][:], note_pair[-1][:, PAIR - 1, :].indirect(listed), ACT.Copy)
        for t in range(PACK - 1):
            nc.vector.tensor_tensor(
                diff[t // PAIR][:, t % PAIR, :], key_plane[t][:].indirect(idx[:]), picked[t][:], ALU.subtract
            )
            if t == PAIR - 1:
                absolute(0)

        last_keys = sb.tile([P, I - SCALAR_FROM], F32, name="last_keys")
        nc.scalar.activation(last_keys[:], key_plane[-1][:].indirect(list_slice(idx, SCALAR_FROM, I)), ACT.Copy)
        for a, b in CHUNKS:
            if b <= SCALAR_FROM:
                nc.vector.tensor_tensor(
                    diff[-1][:, PAIR - 1, a:b],
                    key_plane[-1][:].indirect(list_slice(idx, a, b)),
                    last_notes(a, b),
                    ALU.subtract,
                )
        nc.vector.tensor_tensor(
            diff[-1][:, PAIR - 1, SCALAR_FROM:I], last_keys[:], last_notes(SCALAR_FROM, I), ALU.subtract
        )

        q_bf = sb.tile([P, Q, PACK], BF16, name="q_bf", tag="picked_last0", align_bytes=64)
        q_codes = sb.tile([P, Q], U32, name="q_codes", align_bytes=64)
        q_scales = sb.tile([P, Q], U8, name="q_scales", align_bytes=64)
        nc.vector.tensor_copy(
            out=q_bf[:].rearrange("p (c i) t -> p c t i", i=LINE),
            in_=q_raw[:].rearrange("p t (c i) -> p c t i", i=LINE),
        )
        nc.vector.quantize_mx(
            out=q_codes[:].bitcast(FP8X4), scales=q_scales[:], in_=q_bf[:].rearrange("p q t -> p (q t)")
        )

        absolute(1)

        scores = []
        for c, (a, b) in enumerate(CHUNKS):
            codes = sb.tile([P, b - a], U32, name=f"codes{c}", align_bytes=64)
            scales = sb.tile([P, b - a], U8, name=f"scales{c}", align_bytes=64)
            nc.vector.quantize_mx(
                out=codes[:].bitcast(FP8X4), scales=scales[:], in_=zk[c][:].rearrange("p s t -> p (s t)")
            )
            score = ps.tile([P, b - a], F32, name=f"score{c}", tag=f"bank{c}")
            nc.tensor.matmul_mx(
                out=score[:],
                lhsT=q_codes[:].bitcast(FP8X4),
                lhsT_scale=q_scales[:],
                rhs=codes[:].bitcast(FP8X4),
                rhs_scale=scales[:],
                start=True,
                stop=True,
            )
            scores.append(score)

        sums = sb.tile([P, G], F32, name="sums")
        for c, (a, b) in enumerate(CHUNKS):
            weighted = sb.tile([P, b - a], F32, name=f"weighted{c}")
            nc.vector.scalar_tensor_tensor(weighted[:], scores[c][:], 0.0, worth2[:, a:b], ALU.max, ALU.mult)
            nc.vector.tensor_reduce(
                sums[:, a // RUN : b // RUN],
                weighted[:].rearrange("p (g r) -> p g r", r=RUN),
                mybir.AxisListType.X,
                ALU.add,
            )

        nc.vector.tensor_copy(placed[:].indirect(idx3[:]), sums[:])
        for h, queue in enumerate((nc.scalar, nc.sync)):
            cols = slice(h * M // 2, (h + 1) * M // 2)
            result = sb.tile([P, M // 2], F32, name=f"result{h}")
            nc.vector.tensor_tensor(result[:], old_sb[:, cols], placed[:, cols], ALU.add)
            queue.dma_start(out=out[:, cols], in_=result[:])
